import numpy as np
import ml_dtypes


def mxq(x, axis, fmt="e4m3"):
    dtype, down = {"e4m3": (ml_dtypes.float8_e4m3fn, 7), "e5m2": (ml_dtypes.float8_e5m2, 14)}[fmt]
    v = np.moveaxis(np.asarray(x, np.float32).astype(ml_dtypes.bfloat16).astype(np.float64), axis, -1)
    blocks = v.reshape(v.shape[:-1] + (-1, 32))
    amax = np.abs(blocks).max(-1, keepdims=True)
    byte = np.maximum(np.where(amax > 0, np.frexp(amax)[1] - 1 + 127, 0) - down, 1)
    scale = np.exp2(byte - 127.0)
    codes = (blocks / scale).astype(np.float32).astype(dtype).astype(np.float64)
    return np.moveaxis((codes * scale).reshape(v.shape), -1, axis)


WIDE = False


def mx_kscale(k):
    if not WIDE:
        return np.ones(k)
    levels = np.array([10, -10, 5, -5, 0])
    if k % 512:
        return np.exp2(np.random.permutation(np.resize(levels, k // 32))).repeat(32)
    a = np.empty((k // 512, 16))
    for p in range(k // 512):
        a[p, :8] = np.random.permutation(np.resize(levels, 8))
        for g in range(8):
            far = levels[np.abs(levels - a[p, g]) >= 10]
            a[p, g + 8] = far[np.random.randint(len(far))]
    return np.exp2(a.ravel()).repeat(32)


def f64(x):
    return np.asarray(x).astype(np.float64)


def striped8(idx):
    return np.asarray(idx).reshape(8, -1, 16).transpose(0, 2, 1).reshape(128, -1).astype(np.uint16)


def unstriped8(offs):
    return offs.reshape(8, 16, -1).transpose(0, 2, 1).reshape(8, -1).astype(np.int64)


def pick8(x, idx, run):
    r = np.arange(len(x))
    return x[r[:, None], idx[r % (8 * run) // run]]


E2M1 = np.array([0.0, 0.5, 1.0, 1.5, 2.0, 3.0, 4.0, 6.0, -0.0, -0.5, -1.0, -1.5, -2.0, -3.0, -4.0, -6.0])


def pack_weight(w, fmt):
    k, n = w.shape
    w = f64(np.asarray(w, np.float32).astype(ml_dtypes.bfloat16)).reshape(k // 32, 32, n)
    amax = np.abs(w).max(1)
    if fmt == "e4m3":
        byte = np.frexp(amax)[1] - 1 + 127 - 7
    else:
        mant, ex = np.frexp(amax / 6.0)
        byte = np.where(mant > 0.5, ex, ex - 1) + 127
    byte = np.clip(np.where(amax > 0, byte, 1), 1, 254)
    scaled = (w * np.exp2(127.0 - byte)[:, None, :]).reshape(k, n).astype(np.float32)
    by_word = np.ascontiguousarray(scaled.reshape(k // 512, 128, 4, n).transpose(0, 1, 3, 2))
    if fmt == "e4m3":
        words = by_word.astype(ml_dtypes.float8_e4m3fn).view(np.uint8)
    else:
        c = by_word.astype(ml_dtypes.float4_e2m1fn).view(np.uint8) & 0xF
        words = (c[..., 0::2] | (c[..., 1::2] << 4)).reshape(k // 512, 128, 2 * n)
    return np.ascontiguousarray(words), np.ascontiguousarray(byte.astype(np.uint8).reshape(k // 512, 16, n))


def unpack_weight(words, scales, fmt):
    g, _, n = scales.shape
    words = np.ascontiguousarray(words).reshape(g, 128, n, -1)
    if fmt == "e4m3":
        vals = words.view(ml_dtypes.float8_e4m3fn).astype(np.float64)
    else:
        nib = np.empty((g, 128, n, 4), np.uint8)
        nib[..., 0::2] = words & 0xF
        nib[..., 1::2] = words >> 4
        vals = E2M1[nib]
    vals = vals * np.repeat(np.exp2(scales.astype(np.float64) - 127.0), 8, axis=1)[..., None]
    return vals.transpose(0, 1, 3, 2).reshape(g * 512, n)


D, T, I, Q, E = 512, 1024, 512, 512, 256


def setup_inputs():
    n = np.random.standard_normal
    idx = np.stack([np.random.permutation(T)[:I] for _ in range(8)])
    idx2 = np.stack([np.random.permutation(T)[:I] for _ in range(8)])
    idx3 = np.stack([np.random.permutation(T)[:I] for _ in range(8)])
    idx4 = np.stack([np.random.permutation(T)[:I] for _ in range(8)])
    fd = mx_kscale(D)
    fq = mx_kscale(Q)
    keysp = pack_weight(n((D, T)) / fd[:, None], "e4m3")
    mixp = pack_weight(n((Q, E)) * 1.0 / np.sqrt(Q) / fq[:, None], "e2m1")
    return {
        "query": (n((D, Q)) * 1.0 / np.sqrt(D) * fd[:, None]).astype(np.float32),
        "keys_words": keysp[0],
        "keys_scales": keysp[1],
        "rowf": (np.random.uniform(0.5, 2.0, (Q, 1)) * fq[:, None]).astype(np.float32),
        "mix_words": mixp[0],
        "mix_scales": mixp[1],
        "offs": striped8(idx),
        "offs2": striped8(idx2),
        "offs3": striped8(idx3),
        "offs4": striped8(idx4),
    }


def reference(query, keys_words, keys_scales, rowf, mix_words, mix_scales, offs, offs2, offs3, offs4):
    idx = unstriped8(offs)
    idx2 = unstriped8(offs2)
    idx3 = unstriped8(offs3)
    idx4 = unstriped8(offs4)
    keysu = unpack_weight(keys_words, keys_scales, "e4m3")
    mixu = unpack_weight(mix_words, mix_scales, "e2m1")
    queryq = mxq(f64(query), 0, "e4m3")
    a = queryq.T @ keysu
    lo1 = np.minimum(pick8(a, idx, 64), pick8(a, idx2, 64))
    r = pick8(a, idx, 64) - lo1
    f1 = np.zeros((Q, T))
    f1[np.arange(Q)[:, None], idx[np.arange(Q) % 512 // 64]] = r
    f2 = np.zeros((Q, T))
    f2[np.arange(Q)[:, None], idx2[np.arange(Q) % 512 // 64]] = r
    c1 = a - f1
    c2 = c1 + f2
    g = np.minimum(pick8(c2, idx3, 64), pick8(c2, idx4, 64))
    gw = g * f64(rowf)
    gwq = mxq(gw, 0, "e4m3")
    y = mixu.T @ gwq
    return y

@@ -1,0 +1,187 @@
+from contextlib import ExitStack
+
+import concourse.mybir as mybir
+
+D, T, I, Q, E = 512, 1024, 512, 512, 256
+FLOPS = 2 * D * Q * T + 2 * Q * E * I
+
+F32 = mybir.dt.float32
+BF16 = mybir.dt.bfloat16
+I32 = mybir.dt.int32
+U32 = mybir.dt.uint32
+U16 = mybir.dt.uint16
+U8 = mybir.dt.uint8
+FP8X4 = mybir.dt.float8_e4m3fn_x4
+FP4X4 = mybir.dt.float4_e2m1fn_x4
+ALU = mybir.AluOpType
+ACT = mybir.ActivationFunctionType
+
+P = 128
+PACK = 4
+BANK = 512
+SETS = 2
+
+
+def load_scale_rows(queue, plane, rows):
+    for quad in range(4):
+        queue.dma_start(plane[32 * quad : 32 * quad + 4, :].bitcast(I32), rows[4 * quad : 4 * quad + 4, :].bitcast(I32))
+
+
+def tile_attend_bubbled_one_mixed_kernel(tc, query, keys_words, keys_scales, rowf, mix_words, mix_scales, offs, offs2, offs3, offs4, out):
+    nc = tc.nc
+    with ExitStack() as ctx:
+        keep = ctx.enter_context(tc.tile_pool(name="keep", bufs=1))
+        psum = ctx.enter_context(tc.psum_pool(name="psum", bufs=2))
+
+        lists = [keep.tile([P, I // 16], U16, name="list%d" % n) for n in range(4)]
+        key_plane = keep.tile([P, T], U8, align_bytes=64)
+        mix_plane = keep.tile([P, E], U8, align_bytes=64)
+        nc.vector.memset(key_plane[:].bitcast(U32), 0)
+
+        half = Q // 2
+        q_rows = query.rearrange("(p j) q -> p j q", j=PACK)
+        q_raw = [keep.tile([P, PACK, half], F32, name="q_raw%d" % h) for h in range(2)]
+        key_bytes = keys_words[0].rearrange("p n r -> p (n r)")
+        key_words = [keep.tile([P, BANK], U32, align_bytes=64, name="key_words%d" % h) for h in range(2)]
+        for h in range(2):
+            nc.sync.dma_start(q_raw[h][:], q_rows[:, :, h * half : (h + 1) * half])
+        load_scale_rows(nc.scalar, key_plane, keys_scales[0])
+        for h in range(2):
+            nc.sync.dma_start(key_words[h][:].bitcast(I32), key_bytes[:, h * BANK * PACK : (h + 1) * BANK * PACK].bitcast(I32))
+        for tile_of_list, source in zip(lists, (offs, offs2, offs3, offs4)):
+            nc.sync.dma_start(tile_of_list[:], source)
+        factors = keep.tile([P, PACK], F32)
+        nc.sync.dma_start(factors[:], rowf.rearrange("(p t) o -> p (t o)", t=PACK))
+        mix_bytes = keep.tile([P, 2 * E], U8, align_bytes=64)
+        nc.sync.dma_start(mix_bytes[:].bitcast(I32), mix_words[0].bitcast(I32))
+        nc.vector.memset(mix_plane[:].bitcast(U32), 0)
+        load_scale_rows(nc.sync, mix_plane, mix_scales[0])
+
+        taken = [keep.tile([P, T], F32, name="taken%d" % s) for s in range(SETS)]
+        given = [keep.tile([P, T], F32, name="given%d" % s) for s in range(SETS)]
+        for window in taken + given:
+            nc.vector.memset(window[:], 0.0)
+
+        q_dealt = keep.tile([P, PACK, P, PACK], BF16, align_bytes=64)
+        for h in range(2):
+            nc.vector.tensor_copy(
+                q_dealt[:, :, h * (P // 2) : (h + 1) * (P // 2), :].rearrange("p t m j -> p m j t"),
+                q_raw[h][:].rearrange("p j (m t) -> p m j t", t=PACK),
+            )
+
+        gw = keep.tile([P, I, PACK], BF16, align_bytes=64)
+        halves = [slice(0, I // 2), slice(I // 2, I)]
+        list_halves = [slice(0, I // 32), slice(I // 32, I // 16)]
+        scores, looked, gaps, moved, picked = {}, {}, {}, {}, {}
+
+        def score(t):
+            q_codes = keep.tile([P, P], U32, align_bytes=64, name="q_codes%d" % t)
+            q_plane = keep.tile([P, P], U8, align_bytes=64, name="q_plane%d" % t)
+            nc.vector.quantize_mx(q_codes[:].bitcast(FP8X4), q_plane[:], q_dealt[:, t].rearrange("p m j -> p (m j)"))
+            a = keep.tile([P, T], F32, name="a%d" % t, tag="a%d" % t)
+            for h in range(2):
+                cols = slice(h * BANK, (h + 1) * BANK)
+                acc = psum.tile([P, BANK], F32, name="acc")
+                nc.tensor.matmul_mx(acc[:], lhsT=q_codes[:].bitcast(FP8X4), lhsT_scale=q_plane[:], rhs=key_words[h][:].bitcast(FP8X4), rhs_scale=key_plane[:, cols], start=True, stop=True)
+                if t == 0 and h == 1:
+                    nc.vector.tensor_copy(a[:, cols], acc[:])
+                else:
+                    nc.scalar.copy(a[:, cols], acc[:])
+            scores[t] = a
+
+        def look(t, n, entries, quick):
+            a = scores[t]
+            width = 16 * (entries.stop - entries.start)
+            pair = keep.tile([P, 2 * width], F32, name="pair%d_%d" % (t, n), tag="work%d_%d" % (t, n))
+            first, second = pair[:, 0:width], pair[:, width : 2 * width]
+            nc.scalar.activation(first, a[:].indirect(lists[0][:, entries]), ACT.Copy)
+            if quick:
+                nc.vector.tensor_copy(second, a[:].indirect(lists[1][:, entries]))
+            else:
+                nc.scalar.activation(second, a[:].indirect(lists[1][:, entries]), ACT.Copy)
+            looked[t, n] = (first, second)
+
+        def gap(t, n, entries, quick):
+            first, second = looked[t, n]
+            width = 16 * (entries.stop - entries.start)
+            lead = keep.tile([P, width], F32, name="lead%d_%d" % (t, n), tag="work%d_0" % (t - 1) if t >= 2 else "lead%d_%d" % (t, n))
+            r = keep.tile([P, width], F32, name="r%d_%d" % (t, n))
+            if quick:
+                nc.vector.tensor_tensor(lead[:], first, second, ALU.subtract)
+                nc.vector.tensor_scalar(r[:], lead[:], 0.0, None, ALU.max)
+            else:
+                nc.gpsimd.tensor_tensor(lead[:], first, second, ALU.subtract)
+                nc.scalar.activation(r[:], lead[:], ACT.Relu)
+            gaps.setdefault(t, []).append((r, entries))
+
+        def move(t):
+            f1, f2 = taken[t % 2], given[1 if t == 1 else 0]
+            for r, entries in gaps[t]:
+                nc.vector.tensor_copy(f1[:].indirect(lists[0][:, entries]), r[:])
+                nc.vector.tensor_copy(f2[:].indirect(lists[1][:, entries]), r[:])
+            c1 = keep.tile([P, T], F32, name="c1_%d" % t, tag="work%d_0" % (t + 1))
+            c2 = keep.tile([P, T], F32, name="c2_%d" % t, tag="c2_%d" % t)
+            nc.gpsimd.tensor_tensor(c1[:], scores[t][:], f1[:], ALU.subtract)
+            (nc.vector if t == PACK - 1 else nc.gpsimd).tensor_tensor(c2[:], c1[:], f2[:], ALU.add)
+            moved[t] = (c1, c2)
+
+        def pick(t, n, slots, entries):
+            c2 = moved[t][1]
+            width = slots.stop - slots.start
+            pair = keep.tile([P, 2 * width], F32, name="picked%d_%d" % (t, n), tag="work1_0" if t == 0 else "picked%d_%d" % (t, n))
+            third, fourth = pair[:, 0:width], pair[:, width : 2 * width]
+            nc.scalar.activation(third, c2[:].indirect(lists[2][:, entries]), ACT.Copy)
+            nc.scalar.activation(fourth, c2[:].indirect(lists[3][:, entries]), ACT.Copy)
+            picked[t, n] = (third, fourth)
+
+        def weigh(t, n, slots, g):
+            third, fourth = picked[t, n]
+            nc.vector.tensor_tensor(g, third, fourth, ALU.min)
+            if t < 2:
+                nc.scalar.activation(gw[:, slots, t], g, ACT.Copy, scale=factors[:, t : t + 1])
+            else:
+                nc.vector.tensor_scalar(gw[:, slots, t], g, factors[:, t : t + 1], None, ALU.mult)
+
+        whole, whole_list = slice(0, I), slice(0, I // 16)
+        score(0)
+        for n in range(2):
+            look(0, n, list_halves[n], n == 0)
+            gap(0, n, list_halves[n], n == 0)
+        score(1)
+        look(1, 0, whole_list, False)
+        gap(1, 0, whole_list, False)
+        for t in (2, 3):
+            score(t)
+            look(t, 0, whole_list, False)
+        move(0)
+        gap(2, 0, whole_list, False)
+        move(1)
+        pick(0, 0, whole, whole_list)
+        pick(1, 0, whole, whole_list)
+        gap(3, 0, whole_list, False)
+        move(2)
+        g01 = keep.tile([P, T], F32, tag="c2_1")
+        weigh(0, 0, whole, g01[:, 0:I])
+        weigh(1, 0, whole, g01[:, I : 2 * I])
+        pick(2, 0, whole, whole_list)
+        move(3)
+        for n in range(2):
+            pick(3, n, halves[n], list_halves[n])
+        spent = moved[3][0]
+        weigh(2, 0, whole, spent[:, 0:I])
+        for n in range(2):
+            slots = halves[n]
+            width = I // 2
+            weigh(3, n, slots, spent[:, I + slots.start : I + slots.stop])
+            gw_codes = keep.tile([P, width], U32, align_bytes=64, name="gw_codes%d" % n)
+            gw_plane = keep.tile([P, width], U8, align_bytes=64, name="gw_plane%d" % n)
+            nc.vector.quantize_mx(gw_codes[:].bitcast(FP8X4), gw_plane[:], gw[:, slots, :].rearrange("p i t -> p (i t)"))
+            for h in range(E // P):
+                acc = psum.tile([P, BANK], F32, name="acc")
+                nc.tensor.matmul_mx(acc[:, 0:width], lhsT=mix_bytes[:, 2 * P * h : 2 * P * (h + 1)].bitcast(FP4X4), lhsT_scale=mix_plane[:, P * h : P * (h + 1)], rhs=gw_codes[:].bitcast(FP8X4), rhs_scale=gw_plane[:], start=True, stop=True)
+                result = keep.tile([P, width], F32, name="result%d_%d" % (n, h))
+                if n == 1 and h == 1:
+                    nc.vector.tensor_copy(result[:], acc[:, 0:width])
+                else:
+                    nc.scalar.copy(result[:], acc[:, 0:width])
+                nc.sync.dma_start(out[P * h : P * (h + 1), slots], result[:])

@@ -1,6 +1,7 @@
 from contextlib import ExitStack
 
 import concourse.mybir as mybir
+from concourse.masks import make_identity
 
 D, T, I, Q, E = 512, 1024, 512, 512, 256
 FLOPS = 2 * D * Q * T + 2 * Q * E * I
@@ -19,7 +20,7 @@ ACT = mybir.ActivationFunctionType
 P = 128
 PACK = 4
 BANK = 512
-SETS = 2
+GROUP = 16
 
 
 def load_scale_rows(queue, plane, rows):
@@ -31,23 +32,22 @@ def tile_attend_bubbled_one_mixed_kernel(tc, query, keys_words, keys_scales, row
     nc = tc.nc
     with ExitStack() as ctx:
         keep = ctx.enter_context(tc.tile_pool(name="keep", bufs=1))
-        psum = ctx.enter_context(tc.psum_pool(name="psum", bufs=2))
+        psum = ctx.enter_context(tc.psum_pool(name="psum", bufs=1))
 
-        lists = [keep.tile([P, I // 16], U16, name="list%d" % n) for n in range(4)]
+        lists = [keep.tile([P, I // GROUP], U16, name="list%d" % n) for n in range(4)]
         key_plane = keep.tile([P, T], U8, align_bytes=64)
         mix_plane = keep.tile([P, E], U8, align_bytes=64)
-        nc.vector.memset(key_plane[:].bitcast(U32), 0)
+        nc.gpsimd.memset(key_plane[:].bitcast(U32), 0)
 
         half = Q // 2
         q_rows = query.rearrange("(p j) q -> p j q", j=PACK)
         q_raw = [keep.tile([P, PACK, half], F32, name="q_raw%d" % h) for h in range(2)]
         key_bytes = keys_words[0].rearrange("p n r -> p (n r)")
-        key_words = [keep.tile([P, BANK], U32, align_bytes=64, name="key_words%d" % h) for h in range(2)]
+        key_words = keep.tile([P, T], U32, align_bytes=64)
         for h in range(2):
             nc.sync.dma_start(q_raw[h][:], q_rows[:, :, h * half : (h + 1) * half])
         load_scale_rows(nc.scalar, key_plane, keys_scales[0])
-        for h in range(2):
-            nc.sync.dma_start(key_words[h][:].bitcast(I32), key_bytes[:, h * BANK * PACK : (h + 1) * BANK * PACK].bitcast(I32))
+        nc.sync.dma_start(key_words[:].bitcast(I32), key_bytes.bitcast(I32))
         for tile_of_list, source in zip(lists, (offs, offs2, offs3, offs4)):
             nc.sync.dma_start(tile_of_list[:], source)
         factors = keep.tile([P, PACK], F32)
@@ -57,131 +57,149 @@ def tile_attend_bubbled_one_mixed_kernel(tc, query, keys_words, keys_scales, row
         nc.vector.memset(mix_plane[:].bitcast(U32), 0)
         load_scale_rows(nc.sync, mix_plane, mix_scales[0])
 
-        taken = [keep.tile([P, T], F32, name="taken%d" % s) for s in range(SETS)]
-        given = [keep.tile([P, T], F32, name="given%d" % s) for s in range(SETS)]
-        for window in taken + given:
-            nc.vector.memset(window[:], 0.0)
+        taken = [keep.tile([P, T], F32, name="taken%d" % s) for s in range(2)]
+        given = [keep.tile([P, T], F32, name="given%d" % s) for s in range(2)]
+        for s, engine in enumerate((nc.vector, nc.gpsimd)):
+            engine.memset(taken[s][:].bitcast(U32), 0)
+            engine.memset(given[s][:].bitcast(U32), 0)
+        identity = keep.tile([P, P], F32)
+        make_identity(nc, identity[:])
 
-        q_dealt = keep.tile([P, PACK, P, PACK], BF16, align_bytes=64)
-        for h in range(2):
-            nc.vector.tensor_copy(
-                q_dealt[:, :, h * (P // 2) : (h + 1) * (P // 2), :].rearrange("p t m j -> p m j t"),
-                q_raw[h][:].rearrange("p j (m t) -> p m j t", t=PACK),
-            )
+        q_first = keep.tile([P, P, PACK], BF16, align_bytes=64)
+        q_rest = keep.tile([P, PACK - 1, P, PACK], BF16, align_bytes=64)
 
-        gw = keep.tile([P, I, PACK], BF16, align_bytes=64)
+        def deal_first(h):
+            rows = slice(h * (P // 2), (h + 1) * (P // 2))
+            nc.vector.tensor_copy(q_first[:, rows, :], q_raw[h][:].rearrange("p j (m t) -> p t m j", t=PACK)[:, 0])
+
+        def deal_rest(h):
+            rows = slice(h * (P // 2), (h + 1) * (P // 2))
+            (nc.vector.tensor_copy if h == 0 else nc.scalar.copy)(q_rest[:, :, rows, :], q_raw[h][:].rearrange("p j (m t) -> p t m j", t=PACK)[:, 1:PACK])
+
+        spare = keep.tile([P, (PACK - 1) * I], F32)
         halves = [slice(0, I // 2), slice(I // 2, I)]
-        list_halves = [slice(0, I // 32), slice(I // 32, I // 16)]
-        scores, looked, gaps, moved, picked = {}, {}, {}, {}, {}
+        scores, gaps, swapped = {}, {}, {}
 
-        def score(t):
+        def entries(n, slots):
+            return lists[n][:, slots.start // GROUP : slots.stop // GROUP]
+
+        def quantize_queries(t):
             q_codes = keep.tile([P, P], U32, align_bytes=64, name="q_codes%d" % t)
             q_plane = keep.tile([P, P], U8, align_bytes=64, name="q_plane%d" % t)
-            nc.vector.quantize_mx(q_codes[:].bitcast(FP8X4), q_plane[:], q_dealt[:, t].rearrange("p m j -> p (m j)"))
-            a = keep.tile([P, T], F32, name="a%d" % t, tag="a%d" % t)
-            for h in range(2):
-                cols = slice(h * BANK, (h + 1) * BANK)
-                acc = psum.tile([P, BANK], F32, name="acc")
-                nc.tensor.matmul_mx(acc[:], lhsT=q_codes[:].bitcast(FP8X4), lhsT_scale=q_plane[:], rhs=key_words[h][:].bitcast(FP8X4), rhs_scale=key_plane[:, cols], start=True, stop=True)
-                if t == 0 and h == 1:
+            dealt = q_first[:] if t == 0 else q_rest[:, t - 1]
+            nc.vector.quantize_mx(q_codes[:].bitcast(FP8X4), q_plane[:], dealt.rearrange("p m j -> p (m j)"))
+            return q_codes, q_plane
+
+        def score(t, q_codes, q_plane):
+            a = keep.tile([P, T], F32, name="a%d" % t)
+            banks = (0, 1, 2, 3) if t == 0 else (3, 2)
+            width = T // len(banks)
+            for n, bank in enumerate(banks):
+                cols = slice(n * width, (n + 1) * width)
+                acc = psum.tile([P, width], F32, name="acc%d_%d" % (t, n), tag="bank%d" % bank)
+                nc.tensor.matmul_mx(acc[:], lhsT=q_codes[:].bitcast(FP8X4), lhsT_scale=q_plane[:], rhs=key_words[:, cols].bitcast(FP8X4), rhs_scale=key_plane[:, cols], start=True, stop=True)
+                if t == 0 and n % 2 == 1:
                     nc.vector.tensor_copy(a[:, cols], acc[:])
                 else:
                     nc.scalar.copy(a[:, cols], acc[:])
             scores[t] = a
+            gaps[t] = keep.tile([P, I], F32, name="r%d" % t)
 
-        def look(t, n, entries, quick):
-            a = scores[t]
-            width = 16 * (entries.stop - entries.start)
-            pair = keep.tile([P, 2 * width], F32, name="pair%d_%d" % (t, n), tag="work%d_%d" % (t, n))
-            first, second = pair[:, 0:width], pair[:, width : 2 * width]
-            nc.scalar.activation(first, a[:].indirect(lists[0][:, entries]), ACT.Copy)
-            if quick:
-                nc.vector.tensor_copy(second, a[:].indirect(lists[1][:, entries]))
-            else:
-                nc.scalar.activation(second, a[:].indirect(lists[1][:, entries]), ACT.Copy)
-            looked[t, n] = (first, second)
+        def look(t, pair, sign):
+            nc.scalar.activation(pair[:, 0:I], scores[t][:].indirect(lists[0][:]), ACT.Copy)
+            nc.scalar.activation(pair[:, I : 2 * I], scores[t][:].indirect(lists[1][:]), ACT.Copy, scale=sign)
 
-        def gap(t, n, entries, quick):
-            first, second = looked[t, n]
-            width = 16 * (entries.stop - entries.start)
-            lead = keep.tile([P, width], F32, name="lead%d_%d" % (t, n), tag="work%d_0" % (t - 1) if t >= 2 else "lead%d_%d" % (t, n))
-            r = keep.tile([P, width], F32, name="r%d_%d" % (t, n))
-            if quick:
-                nc.vector.tensor_tensor(lead[:], first, second, ALU.subtract)
-                nc.vector.tensor_scalar(r[:], lead[:], 0.0, None, ALU.max)
-            else:
-                nc.gpsimd.tensor_tensor(lead[:], first, second, ALU.subtract)
-                nc.scalar.activation(r[:], lead[:], ACT.Relu)
-            gaps.setdefault(t, []).append((r, entries))
+        def gap_by_turns(t, pair):
+            blocks = [slice(c * P, (c + 1) * P) for c in range(I // P)]
+            turned = psum.tile([P, I], F32, name="turned%d" % t, tag="bank0")
+            for block in blocks:
+                nc.tensor.matmul(turned[:, block], lhsT=pair[:, block], rhs=identity[:], is_transpose=True, start=True, stop=False)
+                nc.tensor.matmul(turned[:, block], lhsT=pair[:, I + block.start : I + block.stop], rhs=identity[:], is_transpose=True, start=False, stop=True)
+            r_turned = turned_gaps[:, t - 2]
+            nc.scalar.activation(r_turned, turned[:], ACT.Relu)
+            back = psum.tile([P, I], F32, name="back%d" % t, tag="bank1")
+            for block in blocks:
+                nc.tensor.transpose(back[:, block], r_turned[:, block], identity[:])
+            nc.scalar.copy(gaps[t][:], back[:])
 
         def move(t):
-            f1, f2 = taken[t % 2], given[1 if t == 1 else 0]
-            for r, entries in gaps[t]:
-                nc.vector.tensor_copy(f1[:].indirect(lists[0][:, entries]), r[:])
-                nc.vector.tensor_copy(f2[:].indirect(lists[1][:, entries]), r[:])
-            c1 = keep.tile([P, T], F32, name="c1_%d" % t, tag="work%d_0" % (t + 1))
-            c2 = keep.tile([P, T], F32, name="c2_%d" % t, tag="c2_%d" % t)
-            nc.gpsimd.tensor_tensor(c1[:], scores[t][:], f1[:], ALU.subtract)
-            (nc.vector if t == PACK - 1 else nc.gpsimd).tensor_tensor(c2[:], c1[:], f2[:], ALU.add)
-            moved[t] = (c1, c2)
+            f1, f2 = taken[t % 2], given[t % 2]
+            c1 = spare[:, 0:T]
+            c2 = keep.tile([P, T], F32, name="c2_%d" % t)
+            nc.vector.tensor_copy(f1[:].indirect(lists[0][:]), gaps[t][:])
+            nc.vector.tensor_copy(f2[:].indirect(lists[1][:]), gaps[t][:])
+            nc.gpsimd.tensor_tensor(c1, scores[t][:], f1[:], ALU.subtract)
+            (nc.vector if t == PACK - 1 else nc.gpsimd).tensor_tensor(c2[:], c1, f2[:], ALU.add)
+            swapped[t] = c2
 
-        def pick(t, n, slots, entries):
-            c2 = moved[t][1]
-            width = slots.stop - slots.start
-            pair = keep.tile([P, 2 * width], F32, name="picked%d_%d" % (t, n), tag="work1_0" if t == 0 else "picked%d_%d" % (t, n))
-            third, fourth = pair[:, 0:width], pair[:, width : 2 * width]
-            nc.scalar.activation(third, c2[:].indirect(lists[2][:, entries]), ACT.Copy)
-            nc.scalar.activation(fourth, c2[:].indirect(lists[3][:, entries]), ACT.Copy)
-            picked[t, n] = (third, fourth)
+        def pick(t, slots, third, fourth):
+            nc.scalar.activation(third, swapped[t][:].indirect(entries(2, slots)), ACT.Copy)
+            nc.scalar.activation(fourth, swapped[t][:].indirect(entries(3, slots)), ACT.Copy)
 
-        def weigh(t, n, slots, g):
-            third, fourth = picked[t, n]
-            nc.vector.tensor_tensor(g, third, fourth, ALU.min)
-            if t < 2:
-                nc.scalar.activation(gw[:, slots, t], g, ACT.Copy, scale=factors[:, t : t + 1])
-            else:
-                nc.vector.tensor_scalar(gw[:, slots, t], g, factors[:, t : t + 1], None, ALU.mult)
+        deal_first(0)
+        deal_rest(0)
+        deal_first(1)
+        packed = [quantize_queries(0)]
+        deal_rest(1)
+        packed.extend(quantize_queries(t) for t in range(1, PACK))
 
-        whole, whole_list = slice(0, I), slice(0, I // 16)
-        score(0)
+        score(0, *packed[0])
+        first = [keep.tile([P, I // 2], F32, name="first%d" % n) for n in range(2)]
+        second = [keep.tile([P, I // 2], F32, name="second%d" % n) for n in range(2)]
+        lead = [keep.tile([P, I // 2], F32, name="lead%d" % n) for n in range(2)]
         for n in range(2):
-            look(0, n, list_halves[n], n == 0)
-            gap(0, n, list_halves[n], n == 0)
-        score(1)
-        look(1, 0, whole_list, False)
-        gap(1, 0, whole_list, False)
-        for t in (2, 3):
-            score(t)
-            look(t, 0, whole_list, False)
-        move(0)
-        gap(2, 0, whole_list, False)
-        move(1)
-        pick(0, 0, whole, whole_list)
-        pick(1, 0, whole, whole_list)
-        gap(3, 0, whole_list, False)
-        move(2)
-        g01 = keep.tile([P, T], F32, tag="c2_1")
-        weigh(0, 0, whole, g01[:, 0:I])
-        weigh(1, 0, whole, g01[:, I : 2 * I])
-        pick(2, 0, whole, whole_list)
-        move(3)
+            nc.scalar.activation(first[n][:], scores[0][:].indirect(entries(0, halves[n])), ACT.Copy)
+            nc.vector.tensor_copy(second[n][:], scores[0][:].indirect(entries(1, halves[n])))
         for n in range(2):
-            pick(3, n, halves[n], list_halves[n])
-        spent = moved[3][0]
-        weigh(2, 0, whole, spent[:, 0:I])
+            nc.vector.tensor_tensor(lead[n][:], first[n][:], second[n][:], ALU.subtract)
         for n in range(2):
-            slots = halves[n]
+            nc.vector.tensor_scalar(gaps[0][:, halves[n]], lead[n][:], 0.0, None, ALU.max)
+        score(1, *packed[1])
+        look(1, spare, 1.0)
+        lead1 = keep.tile([P, I], F32)
+        nc.gpsimd.tensor_tensor(lead1[:], spare[:, 0:I], spare[:, I : 2 * I], ALU.subtract)
+        nc.scalar.activation(gaps[1][:], lead1[:], ACT.Relu)
+        turned_gaps = keep.tile([P, 2, I], F32, tag="picked")
+        for t in range(2, PACK):
+            score(t, *packed[t])
+            pair = keep.tile([P, 2 * I], F32, name="pair%d" % t)
+            look(t, pair, -1.0)
+            gap_by_turns(t, pair)
+
+        picked = keep.tile([P, PACK - 1, 2, I], F32, tag="picked")
+        for t in range(PACK - 1):
+            move(t)
+            pick(t, slice(0, I), picked[:, t, 0], picked[:, t, 1])
+        move(PACK - 1)
+        last = [keep.tile([P, 2, I // 2], F32, name="last%d" % n) for n in range(2)]
+        for n, slots in enumerate(halves):
+            pick(PACK - 1, slots, last[n][:, 0], last[n][:, 1])
+
+        g = spare[:].rearrange("p (t i) -> p t i", i=I)
+        for slots in halves:
+            nc.vector.tensor_tensor(g[:, :, slots], picked[:, :, 0, slots], picked[:, :, 1, slots], ALU.min)
+        g_last = keep.tile([P, I // 2], F32)
+        for n, slots in enumerate(halves):
             width = I // 2
-            weigh(3, n, slots, spent[:, I + slots.start : I + slots.stop])
+            planes = keep.tile([P, PACK, width], BF16, name="planes%d" % n)
+            nc.vector.tensor_tensor(g_last[:], last[n][:, 0], last[n][:, 1], ALU.min)
+            for t in range(PACK - 1):
+                if n == 0:
+                    nc.vector.tensor_scalar(planes[:, t], g[:, t, slots], factors[:, t : t + 1], None, ALU.mult)
+                else:
+                    nc.scalar.activation(planes[:, t], g[:, t, slots], ACT.Copy, scale=factors[:, t : t + 1])
+            nc.vector.tensor_scalar(planes[:, PACK - 1], g_last[:], factors[:, PACK - 1 : PACK], None, ALU.mult)
+            gw = keep.tile([P, width, PACK], BF16, align_bytes=64, name="gw%d" % n)
+            nc.vector.tensor_copy(gw[:], planes[:].rearrange("p t i -> p i t"))
             gw_codes = keep.tile([P, width], U32, align_bytes=64, name="gw_codes%d" % n)
             gw_plane = keep.tile([P, width], U8, align_bytes=64, name="gw_plane%d" % n)
-            nc.vector.quantize_mx(gw_codes[:].bitcast(FP8X4), gw_plane[:], gw[:, slots, :].rearrange("p i t -> p (i t)"))
+            nc.vector.quantize_mx(gw_codes[:].bitcast(FP8X4), gw_plane[:], gw[:].rearrange("p i t -> p (i t)"))
             for h in range(E // P):
-                acc = psum.tile([P, BANK], F32, name="acc")
-                nc.tensor.matmul_mx(acc[:, 0:width], lhsT=mix_bytes[:, 2 * P * h : 2 * P * (h + 1)].bitcast(FP4X4), lhsT_scale=mix_plane[:, P * h : P * (h + 1)], rhs=gw_codes[:].bitcast(FP8X4), rhs_scale=gw_plane[:], start=True, stop=True)
+                acc = psum.tile([P, width], F32, name="out%d_%d" % (n, h))
+                nc.tensor.matmul_mx(acc[:], lhsT=mix_bytes[:, 2 * P * h : 2 * P * (h + 1)].bitcast(FP4X4), lhsT_scale=mix_plane[:, P * h : P * (h + 1)], rhs=gw_codes[:].bitcast(FP8X4), rhs_scale=gw_plane[:], start=True, stop=True)
                 result = keep.tile([P, width], F32, name="result%d_%d" % (n, h))
                 if n == 1 and h == 1:
-                    nc.vector.tensor_copy(result[:], acc[:, 0:width])
+                    nc.vector.tensor_copy(result[:], acc[:])
                 else:
-                    nc.scalar.copy(result[:], acc[:, 0:width])
-                nc.sync.dma_start(out[P * h : P * (h + 1), slots], result[:])
+                    nc.scalar.copy(result[:], acc[:])
+                (nc.scalar if n == 1 and h == 0 else nc.sync).dma_start(out[P * h : P * (h + 1), slots], result[:])

from contextlib import ExitStack

import concourse.mybir as mybir
from concourse.masks import make_identity

D, T, I, Q, E = 512, 1024, 512, 512, 256
FLOPS = 2 * D * Q * T + 2 * Q * E * I

F32 = mybir.dt.float32
BF16 = mybir.dt.bfloat16
I32 = mybir.dt.int32
U32 = mybir.dt.uint32
U16 = mybir.dt.uint16
U8 = mybir.dt.uint8
FP8X4 = mybir.dt.float8_e4m3fn_x4
FP4X4 = mybir.dt.float4_e2m1fn_x4
ALU = mybir.AluOpType
ACT = mybir.ActivationFunctionType

P = 128
PACK = 4
BANK = 512
GROUP = 16


def load_scale_rows(queue, plane, rows):
    for quad in range(4):
        queue.dma_start(plane[32 * quad : 32 * quad + 4, :].bitcast(I32), rows[4 * quad : 4 * quad + 4, :].bitcast(I32))


def tile_attend_bubbled_one_mixed_kernel(tc, query, keys_words, keys_scales, rowf, mix_words, mix_scales, offs, offs2, offs3, offs4, out):
    nc = tc.nc
    with ExitStack() as ctx:
        keep = ctx.enter_context(tc.tile_pool(name="keep", bufs=1))
        psum = ctx.enter_context(tc.psum_pool(name="psum", bufs=1))

        lists = [keep.tile([P, I // GROUP], U16, name="list%d" % n) for n in range(4)]
        key_plane = keep.tile([P, T], U8, align_bytes=64)
        mix_plane = keep.tile([P, E], U8, align_bytes=64)
        nc.gpsimd.memset(key_plane[:].bitcast(U32), 0)

        half = Q // 2
        q_rows = query.rearrange("(p j) q -> p j q", j=PACK)
        q_raw = [keep.tile([P, PACK, half], F32, name="q_raw%d" % h) for h in range(2)]
        key_bytes = keys_words[0].rearrange("p n r -> p (n r)")
        key_words = keep.tile([P, T], U32, align_bytes=64)
        for h in range(2):
            nc.sync.dma_start(q_raw[h][:], q_rows[:, :, h * half : (h + 1) * half])
        load_scale_rows(nc.scalar, key_plane, keys_scales[0])
        nc.sync.dma_start(key_words[:].bitcast(I32), key_bytes.bitcast(I32))
        for tile_of_list, source in zip(lists, (offs, offs2, offs3, offs4)):
            nc.sync.dma_start(tile_of_list[:], source)
        factors = keep.tile([P, PACK], F32)
        nc.sync.dma_start(factors[:], rowf.rearrange("(p t) o -> p (t o)", t=PACK))
        mix_bytes = keep.tile([P, 2 * E], U8, align_bytes=64)
        nc.sync.dma_start(mix_bytes[:].bitcast(I32), mix_words[0].bitcast(I32))
        nc.vector.memset(mix_plane[:].bitcast(U32), 0)
        load_scale_rows(nc.sync, mix_plane, mix_scales[0])

        taken = [keep.tile([P, T], F32, name="taken%d" % s) for s in range(2)]
        given = [keep.tile([P, T], F32, name="given%d" % s) for s in range(2)]
        for s, engine in enumerate((nc.vector, nc.gpsimd)):
            engine.memset(taken[s][:].bitcast(U32), 0)
            engine.memset(given[s][:].bitcast(U32), 0)
        identity = keep.tile([P, P], F32)
        make_identity(nc, identity[:])

        q_first = keep.tile([P, P, PACK], BF16, align_bytes=64)
        q_rest = keep.tile([P, PACK - 1, P, PACK], BF16, align_bytes=64)

        def deal_first(h):
            rows = slice(h * (P // 2), (h + 1) * (P // 2))
            nc.vector.tensor_copy(q_first[:, rows, :], q_raw[h][:].rearrange("p j (m t) -> p t m j", t=PACK)[:, 0])

        def deal_rest(h):
            rows = slice(h * (P // 2), (h + 1) * (P // 2))
            (nc.vector.tensor_copy if h == 0 else nc.scalar.copy)(q_rest[:, :, rows, :], q_raw[h][:].rearrange("p j (m t) -> p t m j", t=PACK)[:, 1:PACK])

        spare = keep.tile([P, (PACK - 1) * I], F32)
        halves = [slice(0, I // 2), slice(I // 2, I)]
        scores, gaps, swapped = {}, {}, {}

        def entries(n, slots):
            return lists[n][:, slots.start // GROUP : slots.stop // GROUP]

        def quantize_queries(t):
            q_codes = keep.tile([P, P], U32, align_bytes=64, name="q_codes%d" % t)
            q_plane = keep.tile([P, P], U8, align_bytes=64, name="q_plane%d" % t)
            dealt = q_first[:] if t == 0 else q_rest[:, t - 1]
            nc.vector.quantize_mx(q_codes[:].bitcast(FP8X4), q_plane[:], dealt.rearrange("p m j -> p (m j)"))
            return q_codes, q_plane

        def score(t, q_codes, q_plane):
            a = keep.tile([P, T], F32, name="a%d" % t)
            banks = (0, 1, 2, 3) if t == 0 else (3, 2)
            width = T // len(banks)
            for n, bank in enumerate(banks):
                cols = slice(n * width, (n + 1) * width)
                acc = psum.tile([P, width], F32, name="acc%d_%d" % (t, n), tag="bank%d" % bank)
                nc.tensor.matmul_mx(acc[:], lhsT=q_codes[:].bitcast(FP8X4), lhsT_scale=q_plane[:], rhs=key_words[:, cols].bitcast(FP8X4), rhs_scale=key_plane[:, cols], start=True, stop=True)
                if t == 0 and n % 2 == 1:
                    nc.vector.tensor_copy(a[:, cols], acc[:])
                else:
                    nc.scalar.copy(a[:, cols], acc[:])
            scores[t] = a
            gaps[t] = keep.tile([P, I], F32, name="r%d" % t)

        def look(t, pair, sign):
            nc.scalar.activation(pair[:, 0:I], scores[t][:].indirect(lists[0][:]), ACT.Copy)
            nc.scalar.activation(pair[:, I : 2 * I], scores[t][:].indirect(lists[1][:]), ACT.Copy, scale=sign)

        def gap_by_turns(t, pair):
            blocks = [slice(c * P, (c + 1) * P) for c in range(I // P)]
            turned = psum.tile([P, I], F32, name="turned%d" % t, tag="bank0")
            for block in blocks:
                nc.tensor.matmul(turned[:, block], lhsT=pair[:, block], rhs=identity[:], is_transpose=True, start=True, stop=False)
                nc.tensor.matmul(turned[:, block], lhsT=pair[:, I + block.start : I + block.stop], rhs=identity[:], is_transpose=True, start=False, stop=True)
            r_turned = turned_gaps[:, t - 2]
            nc.scalar.activation(r_turned, turned[:], ACT.Relu)
            back = psum.tile([P, I], F32, name="back%d" % t, tag="bank1")
            for block in blocks:
                nc.tensor.transpose(back[:, block], r_turned[:, block], identity[:])
            nc.scalar.copy(gaps[t][:], back[:])

        def move(t):
            f1, f2 = taken[t % 2], given[t % 2]
            c1 = spare[:, 0:T]
            c2 = keep.tile([P, T], F32, name="c2_%d" % t)
            nc.vector.tensor_copy(f1[:].indirect(lists[0][:]), gaps[t][:])
            nc.vector.tensor_copy(f2[:].indirect(lists[1][:]), gaps[t][:])
            nc.gpsimd.tensor_tensor(c1, scores[t][:], f1[:], ALU.subtract)
            (nc.vector if t == PACK - 1 else nc.gpsimd).tensor_tensor(c2[:], c1, f2[:], ALU.add)
            swapped[t] = c2

        def pick(t, slots, third, fourth):
            nc.scalar.activation(third, swapped[t][:].indirect(entries(2, slots)), ACT.Copy)
            nc.scalar.activation(fourth, swapped[t][:].indirect(entries(3, slots)), ACT.Copy)

        deal_first(0)
        deal_rest(0)
        deal_first(1)
        packed = [quantize_queries(0)]
        deal_rest(1)
        packed.extend(quantize_queries(t) for t in range(1, PACK))

        score(0, *packed[0])
        first = [keep.tile([P, I // 2], F32, name="first%d" % n) for n in range(2)]
        second = [keep.tile([P, I // 2], F32, name="second%d" % n) for n in range(2)]
        lead = [keep.tile([P, I // 2], F32, name="lead%d" % n) for n in range(2)]
        for n in range(2):
            nc.scalar.activation(first[n][:], scores[0][:].indirect(entries(0, halves[n])), ACT.Copy)
            nc.vector.tensor_copy(second[n][:], scores[0][:].indirect(entries(1, halves[n])))
        for n in range(2):
            nc.vector.tensor_tensor(lead[n][:], first[n][:], second[n][:], ALU.subtract)
        for n in range(2):
            nc.vector.tensor_scalar(gaps[0][:, halves[n]], lead[n][:], 0.0, None, ALU.max)
        score(1, *packed[1])
        look(1, spare, 1.0)
        lead1 = keep.tile([P, I], F32)
        nc.gpsimd.tensor_tensor(lead1[:], spare[:, 0:I], spare[:, I : 2 * I], ALU.subtract)
        nc.scalar.activation(gaps[1][:], lead1[:], ACT.Relu)
        turned_gaps = keep.tile([P, 2, I], F32, tag="picked")
        for t in range(2, PACK):
            score(t, *packed[t])
            pair = keep.tile([P, 2 * I], F32, name="pair%d" % t)
            look(t, pair, -1.0)
            gap_by_turns(t, pair)

        picked = keep.tile([P, PACK - 1, 2, I], F32, tag="picked")
        for t in range(PACK - 1):
            move(t)
            pick(t, slice(0, I), picked[:, t, 0], picked[:, t, 1])
        move(PACK - 1)
        last = [keep.tile([P, 2, I // 2], F32, name="last%d" % n) for n in range(2)]
        for n, slots in enumerate(halves):
            pick(PACK - 1, slots, last[n][:, 0], last[n][:, 1])

        g = spare[:].rearrange("p (t i) -> p t i", i=I)
        for slots in halves:
            nc.vector.tensor_tensor(g[:, :, slots], picked[:, :, 0, slots], picked[:, :, 1, slots], ALU.min)
        g_last = keep.tile([P, I // 2], F32)
        for n, slots in enumerate(halves):
            width = I // 2
            planes = keep.tile([P, PACK, width], BF16, name="planes%d" % n)
            nc.vector.tensor_tensor(g_last[:], last[n][:, 0], last[n][:, 1], ALU.min)
            for t in range(PACK - 1):
                if n == 0:
                    nc.vector.tensor_scalar(planes[:, t], g[:, t, slots], factors[:, t : t + 1], None, ALU.mult)
                else:
                    nc.scalar.activation(planes[:, t], g[:, t, slots], ACT.Copy, scale=factors[:, t : t + 1])
            nc.vector.tensor_scalar(planes[:, PACK - 1], g_last[:], factors[:, PACK - 1 : PACK], None, ALU.mult)
            gw = keep.tile([P, width, PACK], BF16, align_bytes=64, name="gw%d" % n)
            nc.vector.tensor_copy(gw[:], planes[:].rearrange("p t i -> p i t"))
            gw_codes = keep.tile([P, width], U32, align_bytes=64, name="gw_codes%d" % n)
            gw_plane = keep.tile([P, width], U8, align_bytes=64, name="gw_plane%d" % n)
            nc.vector.quantize_mx(gw_codes[:].bitcast(FP8X4), gw_plane[:], gw[:].rearrange("p i t -> p (i t)"))
            for h in range(E // P):
                acc = psum.tile([P, width], F32, name="out%d_%d" % (n, h))
                nc.tensor.matmul_mx(acc[:], lhsT=mix_bytes[:, 2 * P * h : 2 * P * (h + 1)].bitcast(FP4X4), lhsT_scale=mix_plane[:, P * h : P * (h + 1)], rhs=gw_codes[:].bitcast(FP8X4), rhs_scale=gw_plane[:], start=True, stop=True)
                result = keep.tile([P, width], F32, name="result%d_%d" % (n, h))
                if n == 1 and h == 1:
                    nc.vector.tensor_copy(result[:], acc[:])
                else:
                    nc.scalar.copy(result[:], acc[:])
                (nc.scalar if n == 1 and h == 0 else nc.sync).dma_start(out[P * h : P * (h + 1), slots], result[:])
